import numpy as np
import ml_dtypes


def mxq(x, axis, fmt="e4m3"):
    dtype, down = {"e4m3": (ml_dtypes.float8_e4m3fn, 7), "e5m2": (ml_dtypes.float8_e5m2, 14)}[fmt]
    v = np.moveaxis(np.asarray(x, np.float32).astype(ml_dtypes.bfloat16).astype(np.float64), axis, -1)
    blocks = v.reshape(v.shape[:-1] + (-1, 32))
    amax = np.abs(blocks).max(-1, keepdims=True)
    byte = np.maximum(np.where(amax > 0, np.frexp(amax)[1] - 1 + 127, 0) - down, 1)
    scale = np.exp2(byte - 127.0)
    codes = (blocks / scale).astype(np.float32).astype(dtype).astype(np.float64)
    return np.moveaxis((codes * scale).reshape(v.shape), -1, axis)


WIDE = False


def mx_kscale(k):
    if not WIDE:
        return np.ones(k)
    levels = np.array([10, -10, 5, -5, 0])
    if k % 512:
        return np.exp2(np.random.permutation(np.resize(levels, k // 32))).repeat(32)
    a = np.empty((k // 512, 16))
    for p in range(k // 512):
        a[p, :8] = np.random.permutation(np.resize(levels, 8))
        for g in range(8):
            far = levels[np.abs(levels - a[p, g]) >= 10]
            a[p, g + 8] = far[np.random.randint(len(far))]
    return np.exp2(a.ravel()).repeat(32)


def f64(x):
    return np.asarray(x).astype(np.float64)


def striped(idx):
    return np.tile(idx.reshape(-1, 16).T, (8, 1)).astype(np.uint16)


def unstriped(offs):
    return offs[:16].T.reshape(-1).astype(np.int64)


def striped8(idx):
    return np.concatenate([x.reshape(-1, 16).T for x in idx]).astype(np.uint16)


def runs(offs, k):
    lists = np.stack([offs[16 * r : 16 * r + 16].T.reshape(-1) for r in range(8)]).astype(np.int64)
    return lists[np.arange(k) % 512 // 64]


def pack_weight(w):
    k, n = w.shape
    w = f64(np.asarray(w, np.float32).astype(ml_dtypes.bfloat16)).reshape(k // 32, 32, n)
    amax = np.abs(w).max(1)
    byte = np.clip(np.where(amax > 0, np.frexp(amax)[1] - 1 + 127 - 7, 1), 1, 254)
    scaled = (w * np.exp2(127.0 - byte)[:, None, :]).reshape(k, n).astype(np.float32)
    words = np.ascontiguousarray(scaled.reshape(k // 512, 128, 4, n).transpose(0, 1, 3, 2)).astype(ml_dtypes.float8_e4m3fn).view(np.uint8)
    return words, np.ascontiguousarray(byte.astype(np.uint8).reshape(k // 512, 16, n))


def unpack_weight(words, scales):
    g, p, n, _ = words.shape
    vals = np.ascontiguousarray(words).view(ml_dtypes.float8_e4m3fn).astype(np.float64) * np.repeat(np.exp2(scales.astype(np.float64) - 127.0), 8, axis=1)[..., None]
    return vals.transpose(0, 1, 3, 2).reshape(g * 512, n)


E2M1 = np.array([0.0, 0.5, 1.0, 1.5, 2.0, 3.0, 4.0, 6.0, -0.0, -0.5, -1.0, -1.5, -2.0, -3.0, -4.0, -6.0])


def pack_fp4(w):
    k, n = w.shape
    w = f64(np.asarray(w, np.float32).astype(ml_dtypes.bfloat16)).reshape(k // 32, 32, n)
    amax = np.abs(w).max(1)
    mant, ex = np.frexp(amax / 6.0)
    byte = np.clip(np.where(amax > 0, np.where(mant > 0.5, ex, ex - 1) + 127, 1), 1, 254)
    scaled = (w * np.exp2(127.0 - byte)[:, None, :]).reshape(k, n).astype(np.float32)
    c = np.ascontiguousarray(scaled.reshape(k // 512, 128, 4, n).transpose(0, 1, 3, 2)).astype(ml_dtypes.float4_e2m1fn).view(np.uint8) & 0xF
    words = (c[..., 0::2] | (c[..., 1::2] << 4)).reshape(k // 512, 128, 2 * n)
    return np.ascontiguousarray(words), np.ascontiguousarray(byte.astype(np.uint8).reshape(k // 512, 16, n))


def unpack_fp4(words, scales):
    g, _, n = scales.shape
    words = np.ascontiguousarray(words).reshape(g, 128, n, 2)
    nib = np.empty((g, 128, n, 4), np.uint8)
    nib[..., 0::2] = words & 0xF
    nib[..., 1::2] = words >> 4
    vals = E2M1[nib] * np.repeat(np.exp2(scales.astype(np.float64) - 127.0), 8, axis=1)[..., None]
    return vals.transpose(0, 1, 3, 2).reshape(g * 512, n)


def planes(y):
    n, m = y.shape
    v = y.astype(np.float32).astype(ml_dtypes.bfloat16).astype(np.float64).reshape(n // 32, 32, m)
    top = np.abs(v).max(1)
    byte = np.clip(np.where(top > 0, np.frexp(top)[1] - 1 + 127 - 7, 1), 1, 254)
    codes = (v * np.exp2(127.0 - byte)[:, None, :]).reshape(n, m).astype(np.float32).astype(ml_dtypes.float8_e4m3fn).view(np.uint8)
    words = codes.reshape(n // 512, 128, 4, m).transpose(0, 1, 3, 2)
    return np.ascontiguousarray(words), np.ascontiguousarray(byte.astype(np.uint8).reshape(n // 512, 16, m))


K, T, S, H = 512, 2048, 512, 512


def setup_inputs():
    n = np.random.standard_normal
    s = mx_kscale(K)[:, None]
    u = mx_kscale(H)
    packed_xT = pack_weight(n((K, T)) * s)
    packed_w1 = pack_fp4(n((K, H)) / np.sqrt(K) / s)
    packed_w2 = pack_fp4(n((H, H)) / np.sqrt(H) / u[:, None])
    return {
        "x_words": packed_xT[0],
        "x_scales": packed_xT[1],
        "w1_words": packed_w1[0],
        "w1_scales": packed_w1[1],
        "gn": (np.random.uniform(0.5, 1.5, (H, 1)) * u[:, None]).astype(np.float32),
        "w2_words": packed_w2[0],
        "w2_scales": packed_w2[1],
        "offs": striped(np.random.permutation(T)[:S]),
        "nb": striped8(np.stack([np.random.permutation(S) for _ in range(8)])),
    }


def reference(x_words, x_scales, w1_words, w1_scales, gn, w2_words, w2_scales, offs, nb):
    xq = unpack_weight(x_words, x_scales)[:, unstriped(offs)]
    y = unpack_fp4(w1_words, w1_scales).T @ xq
    z = f64(gn) * np.tanh(y)
    w2q = unpack_fp4(w2_words, w2_scales)
    h = np.tanh(y + 0.5 * ((w2q.T @ mxq(z, 0, "e4m3"))))
    z2 = f64(gn) * (h[np.arange(H)[:, None], runs(nb, H)])
    out_0 = np.tanh(y + 0.5 * ((w2q.T @ mxq(z2, 0, "e4m3"))))
    return (out_0,) + planes(out_0)

@@ -1,0 +1,201 @@
+from contextlib import ExitStack
+
+import concourse.mybir as mybir
+
+F32 = mybir.dt.float32
+BF16 = mybir.dt.bfloat16
+I32 = mybir.dt.int32
+U32 = mybir.dt.uint32
+U16 = mybir.dt.uint16
+U8 = mybir.dt.uint8
+FP8X4 = mybir.dt.float8_e4m3fn_x4
+FP4X4 = mybir.dt.float4_e2m1fn_x4
+TANH = mybir.ActivationFunctionType.Tanh
+COPY = mybir.ActivationFunctionType.Copy
+MULT = mybir.AluOpType.mult
+ADD = mybir.AluOpType.add
+
+P = 128
+PACK = 4
+NODES = 2048
+PICKED = 512
+FEATURES = 512
+CHUNK = 128
+CHUNKS = PICKED // CHUNK
+HALF = PICKED // 2
+LIST_COLS = CHUNK // 16
+
+FLOPS = 3 * 2 * FEATURES * FEATURES * PICKED
+
+
+def tile_picked_implicit2_none_po_kernel(
+    tc, x_words, x_scales, w1_words, w1_scales, gn, w2_words, w2_scales, offs, nb, out_0, out_1, out_2
+):
+    nc = tc.nc
+    with ExitStack() as ctx:
+        keep = ctx.enter_context(tc.tile_pool(name="keep", bufs=1))
+        psum = ctx.enter_context(tc.psum_pool(name="psum", bufs=1))
+
+        def sb(name, shape, dtype):
+            return keep.tile(shape, dtype, name=name, align_bytes=64)
+
+        def cols(c):
+            return slice(c * CHUNK, (c + 1) * CHUNK)
+
+        def load_scale_rows(queues, plane, rows):
+            for q in range(4):
+                queues[q].dma_start(out=plane[32 * q : 32 * q + 4, :].bitcast(I32), in_=rows[0, 4 * q : 4 * q + 4, :].bitcast(I32))
+
+        def deal(name, words, scales):
+            dealt_words = sb(name + "_dw", [P, PACK, 2 * P], U8)
+            dealt_scales = sb(name + "_ds", [P, PACK, P], U8)
+            nc.vector.tensor_copy(
+                out=dealt_words[:].rearrange("p t (m b) -> p t m b", b=2),
+                in_=words[:].rearrange("p (m t b) -> p t m b", t=PACK, b=2),
+            )
+            nc.vector.tensor_copy(out=dealt_scales[:], in_=scales[:].rearrange("p (m t) -> p t m", t=PACK))
+            return dealt_words, dealt_scales
+
+        def woven(tile):
+            return tile[:].rearrange("p (c i) t -> p c t i", i=4)
+
+        def planar(tile):
+            return tile[:].rearrange("p t (c i) -> p c t i", i=4)
+
+        def quantise(words, scales, c, values):
+            nc.vector.quantize_mx(out=words[:, cols(c)].bitcast(FP8X4), scales=scales[:, cols(c)], in_=values[:].rearrange("p n t -> p (n t)"))
+
+        def product(out, weights, t, words, scales, start, stop):
+            nc.tensor.matmul_mx(
+                out=out, lhsT=weights[0][:, t, :].bitcast(FP4X4), lhsT_scale=weights[1][:, t, :],
+                rhs=words.bitcast(FP8X4), rhs_scale=scales, start=start, stop=stop,
+            )
+
+        offs_sb = sb("offs_sb", [P, PICKED // 16], U16)
+        nb_sb = sb("nb_sb", [P, PICKED // 16], U16)
+        xw = sb("xw", [P, NODES], U32)
+        xs = sb("xs", [P, NODES], U8)
+        w1w = sb("w1w", [P, 2 * FEATURES], U8)
+        w2w = sb("w2w", [P, 2 * FEATURES], U8)
+        w1s = sb("w1s", [P, FEATURES], U8)
+        w2s = sb("w2s", [P, FEATURES], U8)
+        gain = sb("gain", [P, PACK], F32)
+        warm = sb("warm", [P, 2], F32)
+
+        nc.vector.memset(xs[:].bitcast(I32), 0)
+        nc.gpsimd.memset(w1s[:].bitcast(I32), 0)
+        nc.gpsimd.memset(warm[:, 0:1], 0.0)
+        nc.vector.memset(w2s[:].bitcast(I32), 0)
+
+        nc.sync.dma_start(offs_sb[:], offs)
+        nc.sync.dma_start(out=w1w[:].bitcast(I32), in_=w1_words[0].bitcast(I32))
+        nc.sync.dma_start(out=xw[:].bitcast(I32), in_=x_words[0].rearrange("p n t -> p (n t)").bitcast(I32))
+        load_scale_rows([nc.sync] * 4, xs, x_scales)
+        load_scale_rows([nc.gpsimd, nc.gpsimd, nc.scalar, nc.scalar], w1s, w1_scales)
+        nc.scalar.dma_start(out=gain[:], in_=gn.rearrange("(p t) o -> p (t o)", t=PACK))
+        nc.scalar.activation(out=warm[:, 1:2], in_=warm[:, 0:1], func=TANH)
+        nc.sync.dma_start(nb_sb[:], nb)
+        load_scale_rows([nc.sync] * 4, w2s, w2_scales)
+        nc.sync.dma_start(out=w2w[:].bitcast(I32), in_=w2_words[0].bitcast(I32))
+
+        picked_scales = sb("picked_scales", [P, PICKED], U8)
+        nc.vector.tensor_copy(out=picked_scales[:], in_=xs[:].indirect(offs_sb[:]))
+        w1 = deal("w1", w1w, w1s)
+        picked_words = [sb(f"picked_words{h}", [P, HALF], U32) for h in range(2)]
+        for h in range(2):
+            nc.vector.tensor_copy(out=picked_words[h][:], in_=xw[:].indirect(offs_sb[:, h * (HALF // 16) : (h + 1) * (HALF // 16)]))
+        w2 = deal("w2", w2w, w2s)
+
+        half_gain = sb("half_gain", [P, PACK], F32)
+        half_gain_rows = sb("half_gain_rows", [P, PACK, CHUNK], F32)
+        nc.scalar.activation(out=half_gain[:], in_=gain[:], func=COPY, scale=0.5)
+        nc.scalar.activation(out=half_gain_rows[:], in_=gain[:].unsqueeze(2).to_broadcast([P, PACK, CHUNK]), func=COPY, scale=0.5)
+
+        def picked(c):
+            return picked_words[c // 2][:, cols(c % 2)], picked_scales[:, cols(c)]
+
+        y = sb("y", [P, PACK, PICKED], F32)
+        z_words = sb("z_words", [P, PICKED], U32)
+        z_scales = sb("z_scales", [P, PICKED], U8)
+        round1 = [psum.tile([P, PICKED], F32, name=f"round1_{t}", tag=f"plane{t}") for t in range(PACK)]
+        y_banks, z = [], []
+
+        def first_round_products(c):
+            quantise(z_words, z_scales, c, z[c])
+            for t in range(PACK):
+                product(round1[t][:, cols(c)], w2, t, z_words[:, cols(c)], z_scales[:, cols(c)], True, True)
+
+        for c in range(CHUNKS):
+            bank = psum.tile([P, PACK, CHUNK], F32, name=f"y_bank{c}", tag=f"chunk{c}")
+            y_banks.append(bank)
+            for t in range(PACK):
+                product(bank[:, t, :], w1, t, *picked(c), True, True)
+            tanh_y = sb(f"tanh_y{c}", [P, CHUNK, PACK], F32)
+            nc.scalar.activation(out=tanh_y[:], in_=bank[:].rearrange("p t n -> p n t"), func=TANH)
+            z.append(sb(f"z{c}", [P, CHUNK, PACK], BF16))
+            nc.vector.tensor_tensor(out=z[c][:], in0=tanh_y[:], in1=half_gain[:].unsqueeze(1).to_broadcast([P, CHUNK, PACK]), op=MULT)
+            if c > 0:
+                first_round_products(c - 1)
+        first_round_products(CHUNKS - 1)
+        for c in range(CHUNKS):
+            nc.scalar.copy(out=y[:, :, cols(c)], in_=y_banks[c][:])
+
+        h = []
+        for t in range(PACK):
+            pre = sb(f"pre1_{t}", [P, PICKED], F32)
+            nc.vector.tensor_tensor(out=pre[:], in0=round1[t][:], in1=y[:, t, :], op=ADD)
+            h.append(sb(f"h{t}", [P, PICKED], F32))
+            nc.scalar.activation(out=h[t][:], in_=pre[:], func=TANH)
+
+        z2_words = sb("z2_words", [P, PICKED], U32)
+        z2_scales = sb("z2_scales", [P, PICKED], U8)
+        out_words = sb("out_words", [P, PICKED], U32)
+        out_scales = sb("out_scales", [P, PICKED], U8)
+        out_rows = out_0.rearrange("(p t) n -> p t n", t=PACK)
+        out_word_rows = out_1[0].rearrange("p n t -> p (n t)").bitcast(I32)
+        last = CHUNKS - 1
+        for c in range(CHUNKS):
+            fetched = sb(f"fetched{c}", [P, PACK, CHUNK], F32)
+            for t in range(PACK):
+                nc.vector.tensor_tensor(
+                    out=fetched[:, t, :], in0=h[t][:].indirect(nb_sb[:, c * LIST_COLS : (c + 1) * LIST_COLS]),
+                    in1=half_gain_rows[:, t, :], op=MULT,
+                )
+            z2 = sb(f"z2_{c}", [P, CHUNK, PACK], BF16)
+            if c == last:
+                nc.vector.tensor_copy(out=woven(z2), in_=planar(fetched))
+            else:
+                nc.scalar.copy(out=woven(z2), in_=planar(fetched))
+            quantise(z2_words, z2_scales, c, z2)
+            result = sb(f"result{c}", [P, PACK, CHUNK], F32)
+            rounded = sb(f"rounded{c}", [P, CHUNK, PACK], BF16)
+            z2_c = (z2_words[:, cols(c)], z2_scales[:, cols(c)])
+            if c == 0:
+                bank = psum.tile([P, PACK, CHUNK], F32, name=f"round2_{c}", tag=f"chunk{c}")
+                for t in range(PACK):
+                    product(bank[:, t, :], w2, t, *z2_c, True, True)
+                pre = sb("pre2", [P, PACK, CHUNK], F32)
+                nc.vector.tensor_tensor(out=pre[:], in0=bank[:], in1=y[:, :, cols(c)], op=ADD)
+                nc.scalar.activation(out=result[:], in_=pre[:], func=TANH)
+                nc.scalar.copy(out=woven(rounded), in_=planar(result))
+            elif c < last:
+                bank = psum.tile([P, PACK, CHUNK], F32, name=f"round2_{c}", tag=f"chunk{c}")
+                for t in range(PACK):
+                    product(bank[:, t, :], w1, t, *picked(c), True, False)
+                    product(bank[:, t, :], w2, t, *z2_c, False, True)
+                nc.scalar.activation(out=result[:], in_=bank[:], func=TANH)
+                nc.scalar.activation(out=rounded[:], in_=bank[:].rearrange("p t n -> p n t"), func=TANH)
+            else:
+                banks = [psum.tile([P, CHUNK], F32, name=f"round2_last{t}", tag=f"plane{t}") for t in range(PACK)]
+                for t in range(PACK):
+                    product(banks[t][:], w1, t, *picked(c), True, False)
+                for t in range(PACK):
+                    product(banks[t][:], w2, t, *z2_c, False, True)
+                    nc.scalar.activation(out=result[:, t, :], in_=banks[t][:], func=TANH)
+                nc.vector.tensor_copy(out=woven(rounded), in_=planar(result))
+            nc.sync.dma_start(out=out_rows[:, :, cols(c)], in_=result[:])
+            quantise(out_words, out_scales, c, rounded)
+            nc.sync.dma_start(out=out_word_rows[:, cols(c)], in_=out_words[:, cols(c)].bitcast(I32))
+        for q in range(4):
+            queue = nc.scalar if q % 2 else nc.sync
+            queue.dma_start(out=out_2[0, 4 * q : 4 * q + 4, :].bitcast(I32), in_=out_scales[32 * q : 32 * q + 4, :].bitcast(I32))

@@ -36,15 +36,15 @@ def tile_picked_implicit2_none_po_kernel(
         keep = ctx.enter_context(tc.tile_pool(name="keep", bufs=1))
         psum = ctx.enter_context(tc.psum_pool(name="psum", bufs=1))
 
-        def sb(name, shape, dtype):
-            return keep.tile(shape, dtype, name=name, align_bytes=64)
+        def sb(name, shape, dtype, tag=None):
+            return keep.tile(shape, dtype, name=name, tag=tag or name, align_bytes=64)
 
         def cols(c):
             return slice(c * CHUNK, (c + 1) * CHUNK)
 
-        def load_scale_rows(queues, plane, rows):
-            for q in range(4):
-                queues[q].dma_start(out=plane[32 * q : 32 * q + 4, :].bitcast(I32), in_=rows[0, 4 * q : 4 * q + 4, :].bitcast(I32))
+        def load_scale_rows(plane, rows, quadrants, queue=nc.sync):
+            for q in quadrants:
+                queue.dma_start(out=plane[32 * q : 32 * q + 4, :].bitcast(I32), in_=rows[0, 4 * q : 4 * q + 4, :].bitcast(I32))
 
         def deal(name, words, scales):
             dealt_words = sb(name + "_dw", [P, PACK, 2 * P], U8)
@@ -75,55 +75,59 @@ def tile_picked_implicit2_none_po_kernel(
         nb_sb = sb("nb_sb", [P, PICKED // 16], U16)
         xw = sb("xw", [P, NODES], U32)
         xs = sb("xs", [P, NODES], U8)
-        w1w = sb("w1w", [P, 2 * FEATURES], U8)
+        ww = sb("ww", [P, 2 * FEATURES], U8)
+        ws = sb("ws", [P, FEATURES], U8)
         w2w = sb("w2w", [P, 2 * FEATURES], U8)
-        w1s = sb("w1s", [P, FEATURES], U8)
         w2s = sb("w2s", [P, FEATURES], U8)
         gain = sb("gain", [P, PACK], F32)
         warm = sb("warm", [P, 2], F32)
 
-        nc.vector.memset(xs[:].bitcast(I32), 0)
-        nc.gpsimd.memset(w1s[:].bitcast(I32), 0)
-        nc.gpsimd.memset(warm[:, 0:1], 0.0)
+        nc.gpsimd.memset(xs[:, : NODES // 2].bitcast(I32), 0)
+        nc.vector.memset(xs[:, NODES // 2 :].bitcast(I32), 0)
+        nc.vector.memset(ws[:].bitcast(I32), 0)
         nc.vector.memset(w2s[:].bitcast(I32), 0)
+        nc.vector.memset(warm[:, 0:1], 0.0)
 
         nc.sync.dma_start(offs_sb[:], offs)
-        nc.sync.dma_start(out=w1w[:].bitcast(I32), in_=w1_words[0].bitcast(I32))
-        nc.sync.dma_start(out=xw[:].bitcast(I32), in_=x_words[0].rearrange("p n t -> p (n t)").bitcast(I32))
-        load_scale_rows([nc.sync] * 4, xs, x_scales)
-        load_scale_rows([nc.gpsimd, nc.gpsimd, nc.scalar, nc.scalar], w1s, w1_scales)
-        nc.scalar.dma_start(out=gain[:], in_=gn.rearrange("(p t) o -> p (t o)", t=PACK))
+        nc.sync.dma_start(out=ww[:].bitcast(I32), in_=w1_words[0].bitcast(I32))
+        load_scale_rows(xs, x_scales, [0, 1])
+        load_scale_rows(xs, x_scales, [2, 3], nc.scalar)
         nc.scalar.activation(out=warm[:, 1:2], in_=warm[:, 0:1], func=TANH)
-        nc.sync.dma_start(nb_sb[:], nb)
-        load_scale_rows([nc.sync] * 4, w2s, w2_scales)
+        nc.sync.dma_start(out=xw[:].bitcast(I32), in_=x_words[0].rearrange("p n t -> p (n t)").bitcast(I32))
+        load_scale_rows(ws, w1_scales, range(4))
         nc.sync.dma_start(out=w2w[:].bitcast(I32), in_=w2_words[0].bitcast(I32))
+        load_scale_rows(w2s, w2_scales, range(4))
+        nc.sync.dma_start(out=gain[:], in_=gn.rearrange("(p t) o -> p (t o)", t=PACK))
+        nc.sync.dma_start(nb_sb[:], nb)
 
         picked_scales = sb("picked_scales", [P, PICKED], U8)
         nc.vector.tensor_copy(out=picked_scales[:], in_=xs[:].indirect(offs_sb[:]))
-        w1 = deal("w1", w1w, w1s)
-        picked_words = [sb(f"picked_words{h}", [P, HALF], U32) for h in range(2)]
+        w1 = deal("w1", ww, ws)
+        picked_words = [sb(f"picked_words{h}", [P, HALF], U32, "ws" if h else None) for h in range(2)]
         for h in range(2):
             nc.vector.tensor_copy(out=picked_words[h][:], in_=xw[:].indirect(offs_sb[:, h * (HALF // 16) : (h + 1) * (HALF // 16)]))
         w2 = deal("w2", w2w, w2s)
 
-        half_gain = sb("half_gain", [P, PACK], F32)
         half_gain_rows = sb("half_gain_rows", [P, PACK, CHUNK], F32)
-        nc.scalar.activation(out=half_gain[:], in_=gain[:], func=COPY, scale=0.5)
         nc.scalar.activation(out=half_gain_rows[:], in_=gain[:].unsqueeze(2).to_broadcast([P, PACK, CHUNK]), func=COPY, scale=0.5)
 
         def picked(c):
             return picked_words[c // 2][:, cols(c % 2)], picked_scales[:, cols(c)]
 
-        y = sb("y", [P, PACK, PICKED], F32)
+        last = CHUNKS - 1
+        repeated = (0, 1)
+        added = (2, 3)
         z_words = sb("z_words", [P, PICKED], U32)
         z_scales = sb("z_scales", [P, PICKED], U8)
         round1 = [psum.tile([P, PICKED], F32, name=f"round1_{t}", tag=f"plane{t}") for t in range(PACK)]
         y_banks, z = [], []
 
         def first_round_products(c):
+            for t in repeated:
+                product(round1[t][:, cols(c)], w1, t, *picked(c), True, False)
             quantise(z_words, z_scales, c, z[c])
-            for t in range(PACK):
-                product(round1[t][:, cols(c)], w2, t, z_words[:, cols(c)], z_scales[:, cols(c)], True, True)
+            for t in (2, 0, 3, 1):
+                product(round1[t][:, cols(c)], w2, t, z_words[:, cols(c)], z_scales[:, cols(c)], t in added, True)
 
         for c in range(CHUNKS):
             bank = psum.tile([P, PACK, CHUNK], F32, name=f"y_bank{c}", tag=f"chunk{c}")
@@ -133,19 +137,37 @@ def tile_picked_implicit2_none_po_kernel(
             tanh_y = sb(f"tanh_y{c}", [P, CHUNK, PACK], F32)
             nc.scalar.activation(out=tanh_y[:], in_=bank[:].rearrange("p t n -> p n t"), func=TANH)
             z.append(sb(f"z{c}", [P, CHUNK, PACK], BF16))
-            nc.vector.tensor_tensor(out=z[c][:], in0=tanh_y[:], in1=half_gain[:].unsqueeze(1).to_broadcast([P, CHUNK, PACK]), op=MULT)
+            nc.vector.scalar_tensor_tensor(
+                out=z[c][:], in0=tanh_y[:], scalar=0.5, in1=gain[:].unsqueeze(1).to_broadcast([P, CHUNK, PACK]), op0=MULT, op1=MULT
+            )
             if c > 0:
                 first_round_products(c - 1)
-        first_round_products(CHUNKS - 1)
+        pass
+        y = sb("y", [P, PACK, PICKED], F32)
         for c in range(CHUNKS):
-            nc.scalar.copy(out=y[:, :, cols(c)], in_=y_banks[c][:])
+            nc.scalar.copy(out=y[:, 2:4, cols(c)], in_=y_banks[c][:, 2:4, :])
+        early, late = slice(0, last * CHUNK), cols(last)
+        pre = {t: sb(f"pre1_{t}", [P, PICKED], F32) for t in added}
+        for t in repeated:
+            product(round1[t][:, late], w1, t, *picked(last), True, False)
+        quantise(z_words, z_scales, last, z[last])
+        for t in repeated:
+            product(round1[t][:, late], w2, t, z_words[:, late], z_scales[:, late], False, True)
+        for t in added:
+            nc.vector.tensor_tensor(out=pre[t][:, early], in0=round1[t][:, early], in1=y[:, t, early], op=ADD)
+            product(round1[t][:, late], w2, t, z_words[:, late], z_scales[:, late], True, True)
+        for t in added:
+            nc.vector.tensor_tensor(out=pre[t][:, late], in0=round1[t][:, late], in1=y[:, t, late], op=ADD)
 
-        h = []
+        h = [sb(f"h{t}", [P, PICKED], F32) for t in range(PACK)]
         for t in range(PACK):
-            pre = sb(f"pre1_{t}", [P, PICKED], F32)
-            nc.vector.tensor_tensor(out=pre[:], in0=round1[t][:], in1=y[:, t, :], op=ADD)
-            h.append(sb(f"h{t}", [P, PICKED], F32))
-            nc.scalar.activation(out=h[t][:], in_=pre[:], func=TANH)
+            if t in repeated:
+                nc.scalar.activation(out=h[t][:], in_=round1[t][:], func=TANH)
+            else:
+                nc.scalar.activation(out=h[t][:], in_=pre[t][:], func=TANH)
+            if t == 0:
+                pass
+        pass
 
         z2_words = sb("z2_words", [P, PICKED], U32)
         z2_scales = sb("z2_scales", [P, PICKED], U8)
@@ -153,48 +175,62 @@ def tile_picked_implicit2_none_po_kernel(
         out_scales = sb("out_scales", [P, PICKED], U8)
         out_rows = out_0.rearrange("(p t) n -> p t n", t=PACK)
         out_word_rows = out_1[0].rearrange("p n t -> p (n t)").bitcast(I32)
-        last = CHUNKS - 1
+        def finish(c, bank, result, rounded):
+            pre = sb(f"pre2_{c}", [P, PACK, CHUNK], F32)
+            nc.vector.tensor_tensor(out=pre[:], in0=bank[:], in1=y[:, :, cols(c)], op=ADD)
+            nc.scalar.activation(out=result[:], in_=pre[:], func=TANH)
+            if c in [2,3]:
+                nc.vector.tensor_copy(out=woven(rounded), in_=planar(result))
+            else:
+                nc.scalar.copy(out=woven(rounded), in_=planar(result))
+            nc.sync.dma_start(out=out_rows[:, :, cols(c)], in_=result[:])
+
+        roundeds = []
+        after = {2: 0, 3: 1}
         for c in range(CHUNKS):
-            fetched = sb(f"fetched{c}", [P, PACK, CHUNK], F32)
+            fetched = sb(f"fetched{c}", [P, PACK, CHUNK], F32, f"fetched{c % 2}")
             for t in range(PACK):
                 nc.vector.tensor_tensor(
                     out=fetched[:, t, :], in0=h[t][:].indirect(nb_sb[:, c * LIST_COLS : (c + 1) * LIST_COLS]),
                     in1=half_gain_rows[:, t, :], op=MULT,
                 )
-            z2 = sb(f"z2_{c}", [P, CHUNK, PACK], BF16)
+            if c == 0:
+                pass
             if c == last:
+                pass
+            z2 = sb(f"z2_{c}", [P, CHUNK, PACK], BF16)
+            if c in [3]:
                 nc.vector.tensor_copy(out=woven(z2), in_=planar(fetched))
             else:
                 nc.scalar.copy(out=woven(z2), in_=planar(fetched))
+            if c < last:
+                nc.scalar.copy(out=y[:, 0:2, cols(c)], in_=y_banks[c][:, 0:2, :])
             quantise(z2_words, z2_scales, c, z2)
             result = sb(f"result{c}", [P, PACK, CHUNK], F32)
             rounded = sb(f"rounded{c}", [P, CHUNK, PACK], BF16)
             z2_c = (z2_words[:, cols(c)], z2_scales[:, cols(c)])
-            if c == 0:
+            if c < last:
                 bank = psum.tile([P, PACK, CHUNK], F32, name=f"round2_{c}", tag=f"chunk{c}")
                 for t in range(PACK):
                     product(bank[:, t, :], w2, t, *z2_c, True, True)
-                pre = sb("pre2", [P, PACK, CHUNK], F32)
-                nc.vector.tensor_tensor(out=pre[:], in0=bank[:], in1=y[:, :, cols(c)], op=ADD)
-                nc.scalar.activation(out=result[:], in_=pre[:], func=TANH)
-                nc.scalar.copy(out=woven(rounded), in_=planar(result))
-            elif c < last:
-                bank = psum.tile([P, PACK, CHUNK], F32, name=f"round2_{c}", tag=f"chunk{c}")
-                for t in range(PACK):
-                    product(bank[:, t, :], w1, t, *picked(c), True, False)
-                    product(bank[:, t, :], w2, t, *z2_c, False, True)
-                nc.scalar.activation(out=result[:], in_=bank[:], func=TANH)
-                nc.scalar.activation(out=rounded[:], in_=bank[:].rearrange("p t n -> p n t"), func=TANH)
+                if c == last - 1:
+                    held = (c, bank, result, rounded)
+                else:
+                    finish(c, bank, result, rounded)
             else:
                 banks = [psum.tile([P, CHUNK], F32, name=f"round2_last{t}", tag=f"plane{t}") for t in range(PACK)]
                 for t in range(PACK):
                     product(banks[t][:], w1, t, *picked(c), True, False)
                 for t in range(PACK):
                     product(banks[t][:], w2, t, *z2_c, False, True)
+                finish(*held)
+                for t in range(PACK):
                     nc.scalar.activation(out=result[:, t, :], in_=banks[t][:], func=TANH)
                 nc.vector.tensor_copy(out=woven(rounded), in_=planar(result))
-            nc.sync.dma_start(out=out_rows[:, :, cols(c)], in_=result[:])
-            quantise(out_words, out_scales, c, rounded)
+                nc.sync.dma_start(out=out_rows[:, :, cols(c)], in_=result[:])
+            roundeds.append(rounded)
+        for c in range(CHUNKS):
+            quantise(out_words, out_scales, c, roundeds[c])
             nc.sync.dma_start(out=out_word_rows[:, cols(c)], in_=out_words[:, cols(c)].bitcast(I32))
         for q in range(4):
             queue = nc.scalar if q % 2 else nc.sync

@@ -17,13 +17,18 @@ ADD = mybir.AluOpType.add
 
 P = 128
 PACK = 4
+QUADRANTS = 4
 NODES = 2048
 PICKED = 512
 FEATURES = 512
 CHUNK = 128
 CHUNKS = PICKED // CHUNK
+LAST = CHUNKS - 1
 HALF = PICKED // 2
-LIST_COLS = CHUNK // 16
+OFFSETS_PER_COLUMN = 16
+REPEATED = slice(0, 2)
+ADDED = slice(2, 4)
+LINE = 4
 
 FLOPS = 3 * 2 * FEATURES * FEATURES * PICKED
 
@@ -32,6 +37,8 @@ def tile_picked_implicit2_none_po_kernel(
     tc, x_words, x_scales, w1_words, w1_scales, gn, w2_words, w2_scales, offs, nb, out_0, out_1, out_2
 ):
     nc = tc.nc
+    repeated_planes = range(PACK)[REPEATED]
+    added_planes = range(PACK)[ADDED]
     with ExitStack() as ctx:
         keep = ctx.enter_context(tc.tile_pool(name="keep", bufs=1))
         psum = ctx.enter_context(tc.psum_pool(name="psum", bufs=1))
@@ -42,13 +49,19 @@ def tile_picked_implicit2_none_po_kernel(
         def cols(c):
             return slice(c * CHUNK, (c + 1) * CHUNK)
 
-        def load_scale_rows(plane, rows, quadrants, queue=nc.sync):
+        def entries(lists, start, count):
+            return lists[:, start // OFFSETS_PER_COLUMN : (start + count) // OFFSETS_PER_COLUMN]
+
+        def live_rows(scale_tile, q):
+            return scale_tile[32 * q : 32 * q + 4, :].bitcast(I32)
+
+        def load_scale_rows(scale_tile, rows, quadrants, queue=nc.sync):
             for q in quadrants:
-                queue.dma_start(out=plane[32 * q : 32 * q + 4, :].bitcast(I32), in_=rows[0, 4 * q : 4 * q + 4, :].bitcast(I32))
+                queue.dma_start(out=live_rows(scale_tile, q), in_=rows[0, 4 * q : 4 * q + 4, :].bitcast(I32))
 
         def deal(name, words, scales):
-            dealt_words = sb(name + "_dw", [P, PACK, 2 * P], U8)
-            dealt_scales = sb(name + "_ds", [P, PACK, P], U8)
+            dealt_words = sb(name + "_dealt_words", [P, PACK, 2 * P], U8)
+            dealt_scales = sb(name + "_dealt_scales", [P, PACK, P], U8)
             nc.vector.tensor_copy(
                 out=dealt_words[:].rearrange("p t (m b) -> p t m b", b=2),
                 in_=words[:].rearrange("p (m t b) -> p t m b", t=PACK, b=2),
@@ -56,57 +69,54 @@ def tile_picked_implicit2_none_po_kernel(
             nc.vector.tensor_copy(out=dealt_scales[:], in_=scales[:].rearrange("p (m t) -> p t m", t=PACK))
             return dealt_words, dealt_scales
 
-        def woven(tile):
-            return tile[:].rearrange("p (c i) t -> p c t i", i=4)
+        def weave(copy, woven, planes):
+            copy(out=woven.rearrange("p (c i) t -> p c t i", i=LINE), in_=planes.rearrange("p t (c i) -> p c t i", i=LINE))
 
-        def planar(tile):
-            return tile[:].rearrange("p t (c i) -> p c t i", i=4)
+        def quantise(words, scales, span, woven):
+            nc.vector.quantize_mx(out=words[:, span].bitcast(FP8X4), scales=scales[:, span], in_=woven.rearrange("p n t -> p (n t)"))
 
-        def quantise(words, scales, c, values):
-            nc.vector.quantize_mx(out=words[:, cols(c)].bitcast(FP8X4), scales=scales[:, cols(c)], in_=values[:].rearrange("p n t -> p (n t)"))
-
-        def product(out, weights, t, words, scales, start, stop):
+        def product(out, weights, t, moving, start, stop):
             nc.tensor.matmul_mx(
                 out=out, lhsT=weights[0][:, t, :].bitcast(FP4X4), lhsT_scale=weights[1][:, t, :],
-                rhs=words.bitcast(FP8X4), rhs_scale=scales, start=start, stop=stop,
+                rhs=moving[0].bitcast(FP8X4), rhs_scale=moving[1], start=start, stop=stop,
             )
 
-        offs_sb = sb("offs_sb", [P, PICKED // 16], U16)
-        nb_sb = sb("nb_sb", [P, PICKED // 16], U16)
-        xw = sb("xw", [P, NODES], U32)
-        xs = sb("xs", [P, NODES], U8)
-        ww = sb("ww", [P, 2 * FEATURES], U8)
-        ws = sb("ws", [P, FEATURES], U8)
-        w2w = sb("w2w", [P, 2 * FEATURES], U8)
-        w2s = sb("w2s", [P, FEATURES], U8)
+        offs_sb = sb("offs_sb", [P, PICKED // OFFSETS_PER_COLUMN], U16)
+        nb_sb = sb("nb_sb", [P, PICKED // OFFSETS_PER_COLUMN], U16)
+        x_words_sb = sb("x_words_sb", [P, NODES], U32)
+        x_scales_sb = sb("x_scales_sb", [P, NODES], U8)
+        w1_words_sb = sb("w1_words_sb", [P, 2 * FEATURES], U8)
+        w1_scales_sb = sb("w1_scales_sb", [P, FEATURES], U8)
+        w2_words_sb = sb("w2_words_sb", [P, 2 * FEATURES], U8)
+        w2_scales_sb = sb("w2_scales_sb", [P, FEATURES], U8)
         gain = sb("gain", [P, PACK], F32)
         warm = sb("warm", [P, 2], F32)
 
-        nc.gpsimd.memset(xs[:, : NODES // 2].bitcast(I32), 0)
-        nc.vector.memset(xs[:, NODES // 2 :].bitcast(I32), 0)
-        nc.vector.memset(ws[:].bitcast(I32), 0)
-        nc.vector.memset(w2s[:].bitcast(I32), 0)
+        nc.gpsimd.memset(x_scales_sb[:, : NODES // 2].bitcast(I32), 0)
+        nc.vector.memset(x_scales_sb[:, NODES // 2 :].bitcast(I32), 0)
+        nc.vector.memset(w1_scales_sb[:].bitcast(I32), 0)
+        nc.vector.memset(w2_scales_sb[:].bitcast(I32), 0)
         nc.vector.memset(warm[:, 0:1], 0.0)
 
         nc.sync.dma_start(offs_sb[:], offs)
-        nc.sync.dma_start(out=ww[:].bitcast(I32), in_=w1_words[0].bitcast(I32))
-        load_scale_rows(xs, x_scales, [0, 1])
-        load_scale_rows(xs, x_scales, [2, 3], nc.scalar)
+        nc.sync.dma_start(out=w1_words_sb[:].bitcast(I32), in_=w1_words[0].bitcast(I32))
+        load_scale_rows(x_scales_sb, x_scales, range(0, 2))
+        load_scale_rows(x_scales_sb, x_scales, range(2, 4), nc.scalar)
         nc.scalar.activation(out=warm[:, 1:2], in_=warm[:, 0:1], func=TANH)
-        nc.sync.dma_start(out=xw[:].bitcast(I32), in_=x_words[0].rearrange("p n t -> p (n t)").bitcast(I32))
-        load_scale_rows(ws, w1_scales, range(4))
-        nc.sync.dma_start(out=w2w[:].bitcast(I32), in_=w2_words[0].bitcast(I32))
-        load_scale_rows(w2s, w2_scales, range(4))
+        nc.sync.dma_start(out=x_words_sb[:].bitcast(I32), in_=x_words[0].rearrange("p n t -> p (n t)").bitcast(I32))
+        load_scale_rows(w1_scales_sb, w1_scales, range(QUADRANTS))
+        nc.sync.dma_start(out=w2_words_sb[:].bitcast(I32), in_=w2_words[0].bitcast(I32))
+        load_scale_rows(w2_scales_sb, w2_scales, range(QUADRANTS))
         nc.sync.dma_start(out=gain[:], in_=gn.rearrange("(p t) o -> p (t o)", t=PACK))
         nc.sync.dma_start(nb_sb[:], nb)
 
         picked_scales = sb("picked_scales", [P, PICKED], U8)
-        nc.vector.tensor_copy(out=picked_scales[:], in_=xs[:].indirect(offs_sb[:]))
-        w1 = deal("w1", ww, ws)
-        picked_words = [sb(f"picked_words{h}", [P, HALF], U32, "ws" if h else None) for h in range(2)]
-        for h in range(2):
-            nc.vector.tensor_copy(out=picked_words[h][:], in_=xw[:].indirect(offs_sb[:, h * (HALF // 16) : (h + 1) * (HALF // 16)]))
-        w2 = deal("w2", w2w, w2s)
+        nc.vector.tensor_copy(out=picked_scales[:], in_=x_scales_sb[:].indirect(offs_sb[:]))
+        w1 = deal("w1", w1_words_sb, w1_scales_sb)
+        picked_words = [sb("picked_words0", [P, HALF], U32), sb("picked_words1", [P, HALF], U32, "w1_scales_sb")]
+        for half in range(2):
+            nc.vector.tensor_copy(out=picked_words[half][:], in_=x_words_sb[:].indirect(entries(offs_sb, half * HALF, HALF)))
+        w2 = deal("w2", w2_words_sb, w2_scales_sb)
 
         half_gain_rows = sb("half_gain_rows", [P, PACK, CHUNK], F32)
         nc.scalar.activation(out=half_gain_rows[:], in_=gain[:].unsqueeze(2).to_broadcast([P, PACK, CHUNK]), func=COPY, scale=0.5)
@@ -114,124 +124,111 @@ def tile_picked_implicit2_none_po_kernel(
         def picked(c):
             return picked_words[c // 2][:, cols(c % 2)], picked_scales[:, cols(c)]
 
-        last = CHUNKS - 1
-        repeated = (0, 1)
-        added = (2, 3)
         z_words = sb("z_words", [P, PICKED], U32)
         z_scales = sb("z_scales", [P, PICKED], U8)
         round1 = [psum.tile([P, PICKED], F32, name=f"round1_{t}", tag=f"plane{t}") for t in range(PACK)]
-        y_banks, z = [], []
+        y_banks, tanh_y, z = [], [], []
 
-        def first_round_products(c):
-            for t in repeated:
-                product(round1[t][:, cols(c)], w1, t, *picked(c), True, False)
-            quantise(z_words, z_scales, c, z[c])
-            for t in (2, 0, 3, 1):
-                product(round1[t][:, cols(c)], w2, t, z_words[:, cols(c)], z_scales[:, cols(c)], t in added, True)
+        def quantise_z(c):
+            for t in repeated_planes:
+                product(round1[t][:, cols(c)], w1, t, picked(c), True, False)
+            quantise(z_words, z_scales, cols(c), z[c][:])
+
+        def z_product(t, c):
+            product(round1[t][:, cols(c)], w2, t, (z_words[:, cols(c)], z_scales[:, cols(c)]), t in added_planes, True)
 
         for c in range(CHUNKS):
-            bank = psum.tile([P, PACK, CHUNK], F32, name=f"y_bank{c}", tag=f"chunk{c}")
-            y_banks.append(bank)
+            y_banks.append(psum.tile([P, PACK, CHUNK], F32, name=f"y_bank{c}", tag=f"chunk{c}"))
             for t in range(PACK):
-                product(bank[:, t, :], w1, t, *picked(c), True, True)
-            tanh_y = sb(f"tanh_y{c}", [P, CHUNK, PACK], F32)
-            nc.scalar.activation(out=tanh_y[:], in_=bank[:].rearrange("p t n -> p n t"), func=TANH)
+                product(y_banks[c][:, t, :], w1, t, picked(c), True, True)
+            tanh_y.append(sb(f"tanh_y{c}", [P, CHUNK, PACK], F32))
+            nc.scalar.activation(out=tanh_y[c][:], in_=y_banks[c][:].rearrange("p t n -> p n t"), func=TANH)
+        for c in range(CHUNKS):
             z.append(sb(f"z{c}", [P, CHUNK, PACK], BF16))
             nc.vector.scalar_tensor_tensor(
-                out=z[c][:], in0=tanh_y[:], scalar=0.5, in1=gain[:].unsqueeze(1).to_broadcast([P, CHUNK, PACK]), op0=MULT, op1=MULT
+                out=z[c][:], in0=tanh_y[c][:], scalar=0.5, in1=gain[:].unsqueeze(1).to_broadcast([P, CHUNK, PACK]), op0=MULT, op1=MULT
             )
             if c > 0:
-                first_round_products(c - 1)
-        pass
+                quantise_z(c - 1)
+                for added, repeated in zip(added_planes, repeated_planes):
+                    z_product(added, c - 1)
+                    z_product(repeated, c - 1)
+
         y = sb("y", [P, PACK, PICKED], F32)
         for c in range(CHUNKS):
-            nc.scalar.copy(out=y[:, 2:4, cols(c)], in_=y_banks[c][:, 2:4, :])
-        early, late = slice(0, last * CHUNK), cols(last)
-        pre = {t: sb(f"pre1_{t}", [P, PICKED], F32) for t in added}
-        for t in repeated:
-            product(round1[t][:, late], w1, t, *picked(last), True, False)
-        quantise(z_words, z_scales, last, z[last])
-        for t in repeated:
-            product(round1[t][:, late], w2, t, z_words[:, late], z_scales[:, late], False, True)
-        for t in added:
-            nc.vector.tensor_tensor(out=pre[t][:, early], in0=round1[t][:, early], in1=y[:, t, early], op=ADD)
-            product(round1[t][:, late], w2, t, z_words[:, late], z_scales[:, late], True, True)
-        for t in added:
-            nc.vector.tensor_tensor(out=pre[t][:, late], in0=round1[t][:, late], in1=y[:, t, late], op=ADD)
+            nc.scalar.copy(out=y[:, ADDED, cols(c)], in_=y_banks[c][:, ADDED, :])
+
+        early, late = slice(0, LAST * CHUNK), cols(LAST)
+        round1_sums = {t: sb(f"round1_sum{t}", [P, PICKED], F32) for t in added_planes}
+        quantise_z(LAST)
+        for t in repeated_planes:
+            z_product(t, LAST)
+        for t in added_planes:
+            nc.vector.tensor_tensor(out=round1_sums[t][:, early], in0=round1[t][:, early], in1=y[:, t, early], op=ADD)
+            z_product(t, LAST)
+        for t in added_planes:
+            nc.vector.tensor_tensor(out=round1_sums[t][:, late], in0=round1[t][:, late], in1=y[:, t, late], op=ADD)
 
         h = [sb(f"h{t}", [P, PICKED], F32) for t in range(PACK)]
         for t in range(PACK):
-            if t in repeated:
-                nc.scalar.activation(out=h[t][:], in_=round1[t][:], func=TANH)
-            else:
-                nc.scalar.activation(out=h[t][:], in_=pre[t][:], func=TANH)
-            if t == 0:
-                pass
-        pass
+            source = round1_sums[t] if t in added_planes else round1[t]
+            nc.scalar.activation(out=h[t][:], in_=source[:], func=TANH)
 
         z2_words = sb("z2_words", [P, PICKED], U32)
         z2_scales = sb("z2_scales", [P, PICKED], U8)
         out_words = sb("out_words", [P, PICKED], U32)
         out_scales = sb("out_scales", [P, PICKED], U8)
+        out_woven = sb("out_woven", [P, PICKED, PACK], BF16)
         out_rows = out_0.rearrange("(p t) n -> p t n", t=PACK)
         out_word_rows = out_1[0].rearrange("p n t -> p (n t)").bitcast(I32)
-        def finish(c, bank, result, rounded):
-            pre = sb(f"pre2_{c}", [P, PACK, CHUNK], F32)
-            nc.vector.tensor_tensor(out=pre[:], in0=bank[:], in1=y[:, :, cols(c)], op=ADD)
-            nc.scalar.activation(out=result[:], in_=pre[:], func=TANH)
-            if c in [2,3]:
-                nc.vector.tensor_copy(out=woven(rounded), in_=planar(result))
-            else:
-                nc.scalar.copy(out=woven(rounded), in_=planar(result))
-            nc.sync.dma_start(out=out_rows[:, :, cols(c)], in_=result[:])
 
-        roundeds = []
-        after = {2: 0, 3: 1}
-        for c in range(CHUNKS):
+        def fetch_and_quantise(c):
             fetched = sb(f"fetched{c}", [P, PACK, CHUNK], F32, f"fetched{c % 2}")
             for t in range(PACK):
                 nc.vector.tensor_tensor(
-                    out=fetched[:, t, :], in0=h[t][:].indirect(nb_sb[:, c * LIST_COLS : (c + 1) * LIST_COLS]),
-                    in1=half_gain_rows[:, t, :], op=MULT,
+                    out=fetched[:, t, :], in0=h[t][:].indirect(entries(nb_sb, c * CHUNK, CHUNK)), in1=half_gain_rows[:, t, :], op=MULT
                 )
-            if c == 0:
-                pass
-            if c == last:
-                pass
             z2 = sb(f"z2_{c}", [P, CHUNK, PACK], BF16)
-            if c in [3]:
-                nc.vector.tensor_copy(out=woven(z2), in_=planar(fetched))
-            else:
-                nc.scalar.copy(out=woven(z2), in_=planar(fetched))
-            if c < last:
-                nc.scalar.copy(out=y[:, 0:2, cols(c)], in_=y_banks[c][:, 0:2, :])
-            quantise(z2_words, z2_scales, c, z2)
+            weave(nc.vector.tensor_copy if c in (0, LAST) else nc.scalar.copy, z2[:], fetched[:])
+            if c < LAST:
+                nc.scalar.copy(out=y[:, REPEATED, cols(c)], in_=y_banks[c][:, REPEATED, :])
+            quantise(z2_words, z2_scales, cols(c), z2[:])
+            return z2_words[:, cols(c)], z2_scales[:, cols(c)]
+
+        def round_and_store(c, result):
+            weave(nc.scalar.copy if c < CHUNKS // 2 else nc.vector.tensor_copy, out_woven[:, cols(c), :], result[:])
+            nc.sync.dma_start(out=out_rows[:, :, cols(c)], in_=result[:])
+
+        def add_y_and_finish(c, bank):
+            round2_sum = sb(f"round2_sum{c}", [P, PACK, CHUNK], F32)
             result = sb(f"result{c}", [P, PACK, CHUNK], F32)
-            rounded = sb(f"rounded{c}", [P, CHUNK, PACK], BF16)
-            z2_c = (z2_words[:, cols(c)], z2_scales[:, cols(c)])
-            if c < last:
-                bank = psum.tile([P, PACK, CHUNK], F32, name=f"round2_{c}", tag=f"chunk{c}")
-                for t in range(PACK):
-                    product(bank[:, t, :], w2, t, *z2_c, True, True)
-                if c == last - 1:
-                    held = (c, bank, result, rounded)
-                else:
-                    finish(c, bank, result, rounded)
-            else:
-                banks = [psum.tile([P, CHUNK], F32, name=f"round2_last{t}", tag=f"plane{t}") for t in range(PACK)]
-                for t in range(PACK):
-                    product(banks[t][:], w1, t, *picked(c), True, False)
-                for t in range(PACK):
-                    product(banks[t][:], w2, t, *z2_c, False, True)
-                finish(*held)
-                for t in range(PACK):
-                    nc.scalar.activation(out=result[:, t, :], in_=banks[t][:], func=TANH)
-                nc.vector.tensor_copy(out=woven(rounded), in_=planar(result))
-                nc.sync.dma_start(out=out_rows[:, :, cols(c)], in_=result[:])
-            roundeds.append(rounded)
-        for c in range(CHUNKS):
-            quantise(out_words, out_scales, c, roundeds[c])
-            nc.sync.dma_start(out=out_word_rows[:, cols(c)], in_=out_words[:, cols(c)].bitcast(I32))
-        for q in range(4):
+            nc.vector.tensor_tensor(out=round2_sum[:], in0=bank[:], in1=y[:, :, cols(c)], op=ADD)
+            nc.scalar.activation(out=result[:], in_=round2_sum[:], func=TANH)
+            round_and_store(c, result)
+
+        for c in range(LAST):
+            z2_operand = fetch_and_quantise(c)
+            round2 = psum.tile([P, PACK, CHUNK], F32, name=f"round2_{c}", tag=f"chunk{c}")
+            for t in range(PACK):
+                product(round2[:, t, :], w2, t, z2_operand, True, True)
+            if c < LAST - 1:
+                add_y_and_finish(c, round2)
+
+        z2_operand = fetch_and_quantise(LAST)
+        last_banks = [psum.tile([P, CHUNK], F32, name=f"round2_last{t}", tag=f"plane{t}") for t in range(PACK)]
+        for t in range(PACK):
+            product(last_banks[t][:], w1, t, picked(LAST), True, False)
+        for t in range(PACK):
+            product(last_banks[t][:], w2, t, z2_operand, False, True)
+        add_y_and_finish(LAST - 1, round2)
+        last_result = sb("last_result", [P, PACK, CHUNK], F32)
+        for t in range(PACK):
+            nc.scalar.activation(out=last_result[:, t, :], in_=last_banks[t][:], func=TANH)
+        round_and_store(LAST, last_result)
+
+        for span in (slice(0, HALF), cols(LAST - 1), cols(LAST)):
+            quantise(out_words, out_scales, span, out_woven[:, span, :])
+            nc.sync.dma_start(out=out_word_rows[:, span], in_=out_words[:, span].bitcast(I32))
+        for q in range(QUADRANTS):
             queue = nc.scalar if q % 2 else nc.sync
-            queue.dma_start(out=out_2[0, 4 * q : 4 * q + 4, :].bitcast(I32), in_=out_scales[32 * q : 32 * q + 4, :].bitcast(I32))
+            queue.dma_start(out=out_2[0, 4 * q : 4 * q + 4, :].bitcast(I32), in_=live_rows(out_scales, q))

from contextlib import ExitStack

import concourse.mybir as mybir

F32 = mybir.dt.float32
BF16 = mybir.dt.bfloat16
I32 = mybir.dt.int32
U32 = mybir.dt.uint32
U16 = mybir.dt.uint16
U8 = mybir.dt.uint8
FP8X4 = mybir.dt.float8_e4m3fn_x4
FP4X4 = mybir.dt.float4_e2m1fn_x4
TANH = mybir.ActivationFunctionType.Tanh
COPY = mybir.ActivationFunctionType.Copy
MULT = mybir.AluOpType.mult
ADD = mybir.AluOpType.add

P = 128
PACK = 4
QUADRANTS = 4
NODES = 2048
PICKED = 512
FEATURES = 512
CHUNK = 128
CHUNKS = PICKED // CHUNK
LAST = CHUNKS - 1
HALF = PICKED // 2
OFFSETS_PER_COLUMN = 16
REPEATED = slice(0, 2)
ADDED = slice(2, 4)
LINE = 4

FLOPS = 3 * 2 * FEATURES * FEATURES * PICKED


def tile_picked_implicit2_none_po_kernel(
    tc, x_words, x_scales, w1_words, w1_scales, gn, w2_words, w2_scales, offs, nb, out_0, out_1, out_2
):
    nc = tc.nc
    repeated_planes = range(PACK)[REPEATED]
    added_planes = range(PACK)[ADDED]
    with ExitStack() as ctx:
        keep = ctx.enter_context(tc.tile_pool(name="keep", bufs=1))
        psum = ctx.enter_context(tc.psum_pool(name="psum", bufs=1))

        def sb(name, shape, dtype, tag=None):
            return keep.tile(shape, dtype, name=name, tag=tag or name, align_bytes=64)

        def cols(c):
            return slice(c * CHUNK, (c + 1) * CHUNK)

        def entries(lists, start, count):
            return lists[:, start // OFFSETS_PER_COLUMN : (start + count) // OFFSETS_PER_COLUMN]

        def live_rows(scale_tile, q):
            return scale_tile[32 * q : 32 * q + 4, :].bitcast(I32)

        def load_scale_rows(scale_tile, rows, quadrants, queue=nc.sync):
            for q in quadrants:
                queue.dma_start(out=live_rows(scale_tile, q), in_=rows[0, 4 * q : 4 * q + 4, :].bitcast(I32))

        def deal(name, words, scales):
            dealt_words = sb(name + "_dealt_words", [P, PACK, 2 * P], U8)
            dealt_scales = sb(name + "_dealt_scales", [P, PACK, P], U8)
            nc.vector.tensor_copy(
                out=dealt_words[:].rearrange("p t (m b) -> p t m b", b=2),
                in_=words[:].rearrange("p (m t b) -> p t m b", t=PACK, b=2),
            )
            nc.vector.tensor_copy(out=dealt_scales[:], in_=scales[:].rearrange("p (m t) -> p t m", t=PACK))
            return dealt_words, dealt_scales

        def weave(copy, woven, planes):
            copy(out=woven.rearrange("p (c i) t -> p c t i", i=LINE), in_=planes.rearrange("p t (c i) -> p c t i", i=LINE))

        def quantise(words, scales, span, woven):
            nc.vector.quantize_mx(out=words[:, span].bitcast(FP8X4), scales=scales[:, span], in_=woven.rearrange("p n t -> p (n t)"))

        def product(out, weights, t, moving, start, stop):
            nc.tensor.matmul_mx(
                out=out, lhsT=weights[0][:, t, :].bitcast(FP4X4), lhsT_scale=weights[1][:, t, :],
                rhs=moving[0].bitcast(FP8X4), rhs_scale=moving[1], start=start, stop=stop,
            )

        offs_sb = sb("offs_sb", [P, PICKED // OFFSETS_PER_COLUMN], U16)
        nb_sb = sb("nb_sb", [P, PICKED // OFFSETS_PER_COLUMN], U16)
        x_words_sb = sb("x_words_sb", [P, NODES], U32)
        x_scales_sb = sb("x_scales_sb", [P, NODES], U8)
        w1_words_sb = sb("w1_words_sb", [P, 2 * FEATURES], U8)
        w1_scales_sb = sb("w1_scales_sb", [P, FEATURES], U8)
        w2_words_sb = sb("w2_words_sb", [P, 2 * FEATURES], U8)
        w2_scales_sb = sb("w2_scales_sb", [P, FEATURES], U8)
        gain = sb("gain", [P, PACK], F32)
        warm = sb("warm", [P, 2], F32)

        nc.gpsimd.memset(x_scales_sb[:, : NODES // 2].bitcast(I32), 0)
        nc.vector.memset(x_scales_sb[:, NODES // 2 :].bitcast(I32), 0)
        nc.vector.memset(w1_scales_sb[:].bitcast(I32), 0)
        nc.vector.memset(w2_scales_sb[:].bitcast(I32), 0)
        nc.vector.memset(warm[:, 0:1], 0.0)

        nc.sync.dma_start(offs_sb[:], offs)
        nc.sync.dma_start(out=w1_words_sb[:].bitcast(I32), in_=w1_words[0].bitcast(I32))
        load_scale_rows(x_scales_sb, x_scales, range(0, 2))
        load_scale_rows(x_scales_sb, x_scales, range(2, 4), nc.scalar)
        nc.scalar.activation(out=warm[:, 1:2], in_=warm[:, 0:1], func=TANH)
        nc.sync.dma_start(out=x_words_sb[:].bitcast(I32), in_=x_words[0].rearrange("p n t -> p (n t)").bitcast(I32))
        load_scale_rows(w1_scales_sb, w1_scales, range(QUADRANTS))
        nc.sync.dma_start(out=w2_words_sb[:].bitcast(I32), in_=w2_words[0].bitcast(I32))
        load_scale_rows(w2_scales_sb, w2_scales, range(QUADRANTS))
        nc.sync.dma_start(out=gain[:], in_=gn.rearrange("(p t) o -> p (t o)", t=PACK))
        nc.sync.dma_start(nb_sb[:], nb)

        picked_scales = sb("picked_scales", [P, PICKED], U8)
        nc.vector.tensor_copy(out=picked_scales[:], in_=x_scales_sb[:].indirect(offs_sb[:]))
        w1 = deal("w1", w1_words_sb, w1_scales_sb)
        picked_words = [sb("picked_words0", [P, HALF], U32), sb("picked_words1", [P, HALF], U32, "w1_scales_sb")]
        for half in range(2):
            nc.vector.tensor_copy(out=picked_words[half][:], in_=x_words_sb[:].indirect(entries(offs_sb, half * HALF, HALF)))
        w2 = deal("w2", w2_words_sb, w2_scales_sb)

        half_gain_rows = sb("half_gain_rows", [P, PACK, CHUNK], F32)
        nc.scalar.activation(out=half_gain_rows[:], in_=gain[:].unsqueeze(2).to_broadcast([P, PACK, CHUNK]), func=COPY, scale=0.5)

        def picked(c):
            return picked_words[c // 2][:, cols(c % 2)], picked_scales[:, cols(c)]

        z_words = sb("z_words", [P, PICKED], U32)
        z_scales = sb("z_scales", [P, PICKED], U8)
        round1 = [psum.tile([P, PICKED], F32, name=f"round1_{t}", tag=f"plane{t}") for t in range(PACK)]
        y_banks, tanh_y, z = [], [], []

        def quantise_z(c):
            for t in repeated_planes:
                product(round1[t][:, cols(c)], w1, t, picked(c), True, False)
            quantise(z_words, z_scales, cols(c), z[c][:])

        def z_product(t, c):
            product(round1[t][:, cols(c)], w2, t, (z_words[:, cols(c)], z_scales[:, cols(c)]), t in added_planes, True)

        for c in range(CHUNKS):
            y_banks.append(psum.tile([P, PACK, CHUNK], F32, name=f"y_bank{c}", tag=f"chunk{c}"))
            for t in range(PACK):
                product(y_banks[c][:, t, :], w1, t, picked(c), True, True)
            tanh_y.append(sb(f"tanh_y{c}", [P, CHUNK, PACK], F32))
            nc.scalar.activation(out=tanh_y[c][:], in_=y_banks[c][:].rearrange("p t n -> p n t"), func=TANH)
        for c in range(CHUNKS):
            z.append(sb(f"z{c}", [P, CHUNK, PACK], BF16))
            nc.vector.scalar_tensor_tensor(
                out=z[c][:], in0=tanh_y[c][:], scalar=0.5, in1=gain[:].unsqueeze(1).to_broadcast([P, CHUNK, PACK]), op0=MULT, op1=MULT
            )
            if c > 0:
                quantise_z(c - 1)
                for added, repeated in zip(added_planes, repeated_planes):
                    z_product(added, c - 1)
                    z_product(repeated, c - 1)

        y = sb("y", [P, PACK, PICKED], F32)
        for c in range(CHUNKS):
            nc.scalar.copy(out=y[:, ADDED, cols(c)], in_=y_banks[c][:, ADDED, :])

        early, late = slice(0, LAST * CHUNK), cols(LAST)
        round1_sums = {t: sb(f"round1_sum{t}", [P, PICKED], F32) for t in added_planes}
        quantise_z(LAST)
        for t in repeated_planes:
            z_product(t, LAST)
        for t in added_planes:
            nc.vector.tensor_tensor(out=round1_sums[t][:, early], in0=round1[t][:, early], in1=y[:, t, early], op=ADD)
            z_product(t, LAST)
        for t in added_planes:
            nc.vector.tensor_tensor(out=round1_sums[t][:, late], in0=round1[t][:, late], in1=y[:, t, late], op=ADD)

        h = [sb(f"h{t}", [P, PICKED], F32) for t in range(PACK)]
        for t in range(PACK):
            source = round1_sums[t] if t in added_planes else round1[t]
            nc.scalar.activation(out=h[t][:], in_=source[:], func=TANH)

        z2_words = sb("z2_words", [P, PICKED], U32)
        z2_scales = sb("z2_scales", [P, PICKED], U8)
        out_words = sb("out_words", [P, PICKED], U32)
        out_scales = sb("out_scales", [P, PICKED], U8)
        out_woven = sb("out_woven", [P, PICKED, PACK], BF16)
        out_rows = out_0.rearrange("(p t) n -> p t n", t=PACK)
        out_word_rows = out_1[0].rearrange("p n t -> p (n t)").bitcast(I32)

        def fetch_and_quantise(c):
            fetched = sb(f"fetched{c}", [P, PACK, CHUNK], F32, f"fetched{c % 2}")
            for t in range(PACK):
                nc.vector.tensor_tensor(
                    out=fetched[:, t, :], in0=h[t][:].indirect(entries(nb_sb, c * CHUNK, CHUNK)), in1=half_gain_rows[:, t, :], op=MULT
                )
            z2 = sb(f"z2_{c}", [P, CHUNK, PACK], BF16)
            weave(nc.vector.tensor_copy if c in (0, LAST) else nc.scalar.copy, z2[:], fetched[:])
            if c < LAST:
                nc.scalar.copy(out=y[:, REPEATED, cols(c)], in_=y_banks[c][:, REPEATED, :])
            quantise(z2_words, z2_scales, cols(c), z2[:])
            return z2_words[:, cols(c)], z2_scales[:, cols(c)]

        def round_and_store(c, result):
            weave(nc.scalar.copy if c < CHUNKS // 2 else nc.vector.tensor_copy, out_woven[:, cols(c), :], result[:])
            nc.sync.dma_start(out=out_rows[:, :, cols(c)], in_=result[:])

        def add_y_and_finish(c, bank):
            round2_sum = sb(f"round2_sum{c}", [P, PACK, CHUNK], F32)
            result = sb(f"result{c}", [P, PACK, CHUNK], F32)
            nc.vector.tensor_tensor(out=round2_sum[:], in0=bank[:], in1=y[:, :, cols(c)], op=ADD)
            nc.scalar.activation(out=result[:], in_=round2_sum[:], func=TANH)
            round_and_store(c, result)

        for c in range(LAST):
            z2_operand = fetch_and_quantise(c)
            round2 = psum.tile([P, PACK, CHUNK], F32, name=f"round2_{c}", tag=f"chunk{c}")
            for t in range(PACK):
                product(round2[:, t, :], w2, t, z2_operand, True, True)
            if c < LAST - 1:
                add_y_and_finish(c, round2)

        z2_operand = fetch_and_quantise(LAST)
        last_banks = [psum.tile([P, CHUNK], F32, name=f"round2_last{t}", tag=f"plane{t}") for t in range(PACK)]
        for t in range(PACK):
            product(last_banks[t][:], w1, t, picked(LAST), True, False)
        for t in range(PACK):
            product(last_banks[t][:], w2, t, z2_operand, False, True)
        add_y_and_finish(LAST - 1, round2)
        last_result = sb("last_result", [P, PACK, CHUNK], F32)
        for t in range(PACK):
            nc.scalar.activation(out=last_result[:, t, :], in_=last_banks[t][:], func=TANH)
        round_and_store(LAST, last_result)

        for span in (slice(0, HALF), cols(LAST - 1), cols(LAST)):
            quantise(out_words, out_scales, span, out_woven[:, span, :])
            nc.sync.dma_start(out=out_word_rows[:, span], in_=out_words[:, span].bitcast(I32))
        for q in range(QUADRANTS):
            queue = nc.scalar if q % 2 else nc.sync
            queue.dma_start(out=out_2[0, 4 * q : 4 * q + 4, :].bitcast(I32), in_=live_rows(out_scales, q))
